import numpy as np
import ml_dtypes


def mxq(x, axis, fmt="e4m3"):
    dtype, down = {"e4m3": (ml_dtypes.float8_e4m3fn, 7), "e5m2": (ml_dtypes.float8_e5m2, 14)}[fmt]
    v = np.moveaxis(np.asarray(x, np.float32).astype(ml_dtypes.bfloat16).astype(np.float64), axis, -1)
    blocks = v.reshape(v.shape[:-1] + (-1, 32))
    amax = np.abs(blocks).max(-1, keepdims=True)
    byte = np.maximum(np.where(amax > 0, np.frexp(amax)[1] - 1 + 127, 0) - down, 1)
    scale = np.exp2(byte - 127.0)
    codes = (blocks / scale).astype(np.float32).astype(dtype).astype(np.float64)
    return np.moveaxis((codes * scale).reshape(v.shape), -1, axis)


WIDE = False


def mx_kscale(k):
    if not WIDE:
        return np.ones(k)
    levels = np.array([10, -10, 5, -5, 0])
    if k % 512:
        return np.exp2(np.random.permutation(np.resize(levels, k // 32))).repeat(32)
    a = np.empty((k // 512, 16))
    for p in range(k // 512):
        a[p, :8] = np.random.permutation(np.resize(levels, 8))
        for g in range(8):
            far = levels[np.abs(levels - a[p, g]) >= 10]
            a[p, g + 8] = far[np.random.randint(len(far))]
    return np.exp2(a.ravel()).repeat(32)


def f64(x):
    return np.asarray(x).astype(np.float64)


def striped(idx):
    return np.tile(idx.reshape(-1, 16).T, (8, 1)).astype(np.uint16)


def unstriped(offs):
    return offs[:16].T.reshape(-1).astype(np.int64)


E2M1 = np.array([0.0, 0.5, 1.0, 1.5, 2.0, 3.0, 4.0, 6.0, -0.0, -0.5, -1.0, -1.5, -2.0, -3.0, -4.0, -6.0])


def pack_weight(w, fmt):
    k, n = w.shape
    w = f64(np.asarray(w, np.float32).astype(ml_dtypes.bfloat16)).reshape(k // 32, 32, n)
    amax = np.abs(w).max(1)
    if fmt == "e4m3":
        byte = np.frexp(amax)[1] - 1 + 127 - 7
    else:
        mant, ex = np.frexp(amax / 6.0)
        byte = np.where(mant > 0.5, ex, ex - 1) + 127
    byte = np.clip(np.where(amax > 0, byte, 1), 1, 254)
    scaled = (w * np.exp2(127.0 - byte)[:, None, :]).reshape(k, n).astype(np.float32)
    by_word = np.ascontiguousarray(scaled.reshape(k // 512, 128, 4, n).transpose(0, 1, 3, 2))
    if fmt == "e4m3":
        words = by_word.astype(ml_dtypes.float8_e4m3fn).view(np.uint8)
    else:
        c = by_word.astype(ml_dtypes.float4_e2m1fn).view(np.uint8) & 0xF
        words = (c[..., 0::2] | (c[..., 1::2] << 4)).reshape(k // 512, 128, 2 * n)
    return np.ascontiguousarray(words), np.ascontiguousarray(byte.astype(np.uint8).reshape(k // 512, 16, n))


def unpack_weight(words, scales, fmt):
    g, _, n = scales.shape
    words = np.ascontiguousarray(words).reshape(g, 128, n, -1)
    if fmt == "e4m3":
        vals = words.view(ml_dtypes.float8_e4m3fn).astype(np.float64)
    else:
        nib = np.empty((g, 128, n, 4), np.uint8)
        nib[..., 0::2] = words & 0xF
        nib[..., 1::2] = words >> 4
        vals = E2M1[nib]
    vals = vals * np.repeat(np.exp2(scales.astype(np.float64) - 127.0), 8, axis=1)[..., None]
    return vals.transpose(0, 1, 3, 2).reshape(g * 512, n)


def gelu(v):
    return 0.5 * v * (1.0 + np.tanh(np.sqrt(2.0 / np.pi) * (v + 0.044715 * v**3)))


K, T, S, H, T2, P, N = 1536, 2048, 1024, 512, 2048, 1024, 768

def setup_inputs():
    n = np.random.standard_normal
    s = mx_kscale(K)[:, None]
    u = mx_kscale(H)[:, None]
    tab_words, tab_scales = pack_weight(n((K, T)) * s, "e4m3")
    w2_words, w2_scales = pack_weight(n((H, N)) / np.sqrt(H) / u, "e2m1")
    return {
        "tab_words": tab_words, "tab_scales": tab_scales,
        "offs": striped(np.random.permutation(T)[:S]),
        "offs2": striped(np.random.permutation(T2)[:S]),
        "offs3": striped(np.random.permutation(T2)[:P]),
        "offs4": striped(np.random.permutation(T2)[:P]),
        "w1": (1.4 * n((K, H)) / np.sqrt(K) / s).astype(np.float32),
        "b1": (0.6 * n(H)).astype(np.float32),
        "gain": (np.exp(0.3 * n(H)) * u[:, 0]).astype(np.float32),
        "wgs": np.exp(0.3 * n((128, S))).astype(np.float32),
        "page0": (n((H, T2)) * u).astype(np.float32),
        "w2_words": w2_words, "w2_scales": w2_scales,
        "w3": (n((H, N)) / np.sqrt(H) / u).astype(np.float32),
    }

def reference(tab_words, tab_scales, offs, offs2, offs3, offs4, w1, b1, gain, wgs, page0, w2_words, w2_scales, w3):
    v = unpack_weight(tab_words, tab_scales, "e4m3")[:, unstriped(offs)]
    a = (mxq(f64(w1), 0, "e4m3").T @ v) + f64(b1)[:, None]
    h = f64(gain)[:, None] * (0.5 * a * (1.0 + np.tanh(np.sqrt(2.0 / np.pi) * (a + 0.044715 * a ** 3))))
    before = f64(page0)
    page = before.copy()
    page[:, unstriped(offs2)] = np.tile(f64(wgs), (H // 128, 1)) * h
    x = page[:, unstriped(offs3)] - np.abs(before[:, unstriped(offs4)])
    xq = mxq(x, 0, "e4m3")
    y2 = unpack_weight(w2_words, w2_scales, "e2m1").T @ xq
    y3 = mxq(f64(w3), 0, "e4m3").T @ xq
    return np.maximum(y2, y3)

@@ -1,0 +1,234 @@
+from contextlib import ExitStack
+
+import concourse.mybir as mybir
+
+K, T, S, H, T2, M, N = 1536, 2048, 1024, 512, 2048, 1024, 768
+FLOPS = 2 * K * H * S + 2 * 2 * H * N * M
+
+F32 = mybir.dt.float32
+BF16 = mybir.dt.bfloat16
+I32 = mybir.dt.int32
+U32 = mybir.dt.uint32
+U16 = mybir.dt.uint16
+U8 = mybir.dt.uint8
+FP8X4 = mybir.dt.float8_e4m3fn_x4
+FP4X4 = mybir.dt.float4_e2m1fn_x4
+ACT = mybir.ActivationFunctionType
+ALU = mybir.AluOpType
+
+P = 128
+PACK = 4
+PASSES = K // (P * PACK)
+BANK = 512
+CHUNK = 256
+W3_HALF = N // 2
+
+
+def tile_list_insulator_patrol_scores_kernel(
+    tc, tab_words, tab_scales, offs, offs2, offs3, offs4, w1, b1, gain, wgs, page0, w2_words, w2_scales, w3, out
+):
+    nc = tc.nc
+    with ExitStack() as ctx:
+        keep = ctx.enter_context(tc.tile_pool(name="keep", bufs=1))
+        ring = ctx.enter_context(tc.tile_pool(name="ring", bufs=2))
+        psum = ctx.enter_context(tc.psum_pool(name="psum", bufs=1))
+
+        def load_list(src, name):
+            tile = keep.tile([P, src.shape[1]], U16, name=name)
+            nc.sync.dma_start(tile[:], src)
+            return tile
+
+        def load_table(a):
+            tile = keep.tile([P, T], U32, name=f"table{a}")
+            nc.sync.dma_start(tile[:].bitcast(I32), tab_words[a].rearrange("p t i -> p (t i)").bitcast(I32))
+            return tile
+
+        def load_w1(a):
+            tile = ring.tile([P, PACK, H], F32, name=f"w1_raw{a}", tag="raw", bufs=3)
+            rows = w1[a * P * PACK : (a + 1) * P * PACK, :]
+            nc.sync.dma_start(tile[:], rows.rearrange("(p j) c -> p j c", j=PACK))
+            return tile
+
+        def load_page(t):
+            tile = keep.tile([P, T2], F32, name=f"page{t}")
+            nc.sync.dma_start(tile[:], page0.rearrange("(p t) c -> t p c", t=PACK)[t])
+            return tile
+
+        def load_rows(src, name):
+            tile = keep.tile([P, PACK], F32, name=name)
+            nc.sync.dma_start(tile[:], src.rearrange("(p t) -> p t", t=PACK))
+            return tile
+
+        table_scale = keep.tile([P, T], U8, name="table_scale")
+        w2_scale = keep.tile([P, N], U8, name="w2_scale", align_bytes=64)
+        nc.vector.memset(table_scale[:].bitcast(I32), 0)
+        nc.vector.memset(w2_scale[:].bitcast(I32), 0)
+        for q in range(4):
+            nc.gpsimd.dma_start(
+                table_scale[32 * q : 32 * q + 4 * PASSES, :].bitcast(I32),
+                tab_scales[:, 4 * q : 4 * q + 4, :].bitcast(I32),
+            )
+
+        table, w1_raw, page = {}, {}, {}
+        list1 = load_list(offs, "list1")
+        table[0] = load_table(0)
+        w1_raw[0] = load_w1(0)
+        list4 = load_list(offs4, "list4")
+        page[0] = load_page(0)
+        w1_raw[1] = load_w1(1)
+        table[1] = load_table(1)
+        w1_raw[2] = load_w1(2)
+        table[2] = load_table(2)
+        bias = load_rows(b1, "bias")
+        gains = load_rows(gain, "gains")
+        list2 = load_list(offs2, "list2")
+        page[1] = load_page(1)
+        wgs_rows = wgs.rearrange("(q t) j -> q t j", t=PACK)
+        factor_first = keep.tile([P, S], F32, name="factor_first")
+        factor_rest = keep.tile([P, PACK - 1, S], F32, name="factor_rest")
+        for q in range(4):
+            nc.sync.dma_start(factor_first[32 * q : 32 * (q + 1), :], wgs_rows[:, 0, :])
+        page[2] = load_page(2)
+        for q in range(4):
+            nc.sync.dma_start(factor_rest[32 * q : 32 * (q + 1), :, :], wgs_rows[:, 1:PACK, :])
+        page[3] = load_page(3)
+        factor = [factor_first[:]] + [factor_rest[:, t, :] for t in range(PACK - 1)]
+        list3 = load_list(offs3, "list3")
+        w2_code = keep.tile([P, 2 * N], U8, name="w2_code", align_bytes=64)
+        nc.sync.dma_start(w2_code[:].bitcast(I32), w2_words[0].bitcast(I32))
+        for q in range(4):
+            nc.sync.dma_start(
+                w2_scale[32 * q : 32 * q + 4, :].bitcast(I32), w2_scales[0, 4 * q : 4 * q + 4, :].bitcast(I32)
+            )
+
+        picked = [keep.tile([P, S], U32, name=f"picked{a}", align_bytes=64) for a in range(PASSES)]
+        picked_scale = keep.tile([P, S], U8, name="picked_scale", align_bytes=64)
+        w1_code = [keep.tile([P, H], U32, name=f"w1_code{a}", align_bytes=64) for a in range(PASSES)]
+        w1_scale = [keep.tile([P, H], U8, name=f"w1_scale{a}", align_bytes=64) for a in range(PASSES)]
+        magnitude = [keep.tile([P, M], F32, name=f"magnitude{t}") for t in range(PACK)]
+
+        def gather_table(a):
+            nc.vector.tensor_copy(picked[a][:], table[a][:].indirect(list1[:]))
+
+        def quantise_w1(a):
+            grouped = ring.tile([P, PACK * H], BF16, name=f"w1_grouped{a}", tag="grouped", align_bytes=64)
+            nc.scalar.copy(
+                grouped[:].rearrange("p (t m j) -> p m t j", t=PACK, j=PACK),
+                w1_raw[a][:].rearrange("p j (m t) -> p m t j", t=PACK),
+            )
+            nc.vector.quantize_mx(out=w1_code[a][:].bitcast(FP8X4), scales=w1_scale[a][:], in_=grouped[:])
+
+        def fetch_before(t):
+            before = ring.tile([P, M], F32, name=f"before{t}", tag="before")
+            nc.vector.tensor_copy(before[:], page[t][:].indirect(list4[:]))
+            nc.scalar.activation(magnitude[t][:], before[:], ACT.Abs)
+
+        gather_table(0)
+        nc.vector.tensor_copy(picked_scale[:], table_scale[:].indirect(list1[:]))
+        fetch_before(0)
+        quantise_w1(0)
+        gather_table(1)
+        quantise_w1(1)
+        gather_table(2)
+        quantise_w1(2)
+
+        hidden = {}
+        for t in range(PACK):
+            if t > 0:
+                fetch_before(t)
+            nc.scalar.activation(factor[t], factor[t], ACT.Copy, scale=gains[:, t : t + 1])
+            hidden[t] = ring.tile([P, S], F32, name=f"hidden{t}", tag="hidden")
+            for half in range(S // BANK):
+                cols = slice(half * BANK, (half + 1) * BANK)
+                acc = psum.tile([P, BANK], F32, name=f"acc{t}_{half}", tag="y2", bufs=4)
+                for a in range(PASSES):
+                    nc.tensor.matmul_mx(
+                        out=acc[:],
+                        lhsT=w1_code[a][:, t * P : (t + 1) * P].bitcast(FP8X4),
+                        lhsT_scale=w1_scale[a][:, t * P : (t + 1) * P],
+                        rhs=picked[a][:, cols].bitcast(FP8X4),
+                        rhs_scale=picked_scale[4 * a : P, cols],
+                        start=(a == 0),
+                        stop=(a == PASSES - 1),
+                    )
+                nc.scalar.activation(hidden[t][:, cols], acc[:], ACT.Gelu_apprx_tanh, bias=bias[:, t : t + 1])
+            nc.vector.tensor_tensor(page[t][:].indirect(list2[:]), hidden[t][:], factor[t], ALU.mult)
+
+        w3_code, w3_scale = [], []
+        for u in range(2):
+            raw = ring.tile([P, PACK, W3_HALF], F32, name=f"w3_raw{u}", tag="raw", bufs=3)
+            nc.sync.dma_start(
+                raw[:], w3[:, u * W3_HALF : (u + 1) * W3_HALF].rearrange("(p j) c -> p j c", j=PACK)
+            )
+            grouped = ring.tile([P, PACK * W3_HALF], BF16, name=f"w3_grouped{u}", tag="grouped", align_bytes=64)
+            nc.scalar.copy(grouped[:].rearrange("p (c j) -> p c j", j=PACK), raw[:].rearrange("p j c -> p c j"))
+            code = keep.tile([P, W3_HALF], U32, name=f"w3_code{u}", align_bytes=64)
+            scale = keep.tile([P, W3_HALF], U8, name=f"w3_scale{u}", align_bytes=64)
+            nc.vector.quantize_mx(out=code[:].bitcast(FP8X4), scales=scale[:], in_=grouped[:])
+            w3_code.append(code)
+            w3_scale.append(scale)
+
+        chunks = M // CHUNK
+        diff = [hidden[PACK - 1][:], factor[PACK - 1]]
+        out_rows = out.rearrange("(b u p) m -> b p u m", u=2, p=P)
+        x_code, x_scale, x_grouped = {}, {}, {}
+
+        def fetch_after(c):
+            for t in range(PACK):
+                nc.vector.tensor_tensor(
+                    diff[c % 2][:, t * CHUNK : (t + 1) * CHUNK],
+                    page[t][:].indirect(list3[:, c * CHUNK // 16 : (c + 1) * CHUNK // 16]),
+                    magnitude[t][:, c * CHUNK : (c + 1) * CHUNK],
+                    ALU.subtract,
+                )
+            x_grouped[c] = ring.tile([P, PACK * CHUNK], BF16, name=f"x_grouped{c}", tag="x_grouped", align_bytes=64)
+            nc.scalar.copy(
+                x_grouped[c][:].rearrange("p (m t) -> p m t", t=PACK),
+                diff[c % 2].rearrange("p (t m) -> p m t", t=PACK),
+            )
+
+        def quantise_x(c):
+            x_code[c] = ring.tile([P, CHUNK], U32, name=f"x_code{c}", tag="x_code", align_bytes=64)
+            x_scale[c] = ring.tile([P, CHUNK], U8, name=f"x_scale{c}", tag="x_scale", align_bytes=64)
+            nc.vector.quantize_mx(out=x_code[c][:].bitcast(FP8X4), scales=x_scale[c][:], in_=x_grouped[c][:])
+
+        def scores(c):
+            for b in range(N // (2 * P)):
+                y2 = psum.tile([P, 2, CHUNK], F32, name=f"y2_{c}_{b}", tag="y2", bufs=4)
+                y3 = psum.tile([P, 2, CHUNK], F32, name=f"y3_{c}_{b}", tag="y3", bufs=4)
+                for u in range(2):
+                    n = 2 * b + u
+                    nc.tensor.matmul_mx(
+                        out=y2[:, u, :],
+                        lhsT=w2_code[:, 2 * P * n : 2 * P * (n + 1)].bitcast(FP4X4),
+                        lhsT_scale=w2_scale[:, P * n : P * (n + 1)],
+                        rhs=x_code[c][:].bitcast(FP8X4),
+                        rhs_scale=x_scale[c][:],
+                        start=True,
+                        stop=True,
+                    )
+                for u in range(2):
+                    half, n = divmod(2 * b + u, W3_HALF // P)
+                    nc.tensor.matmul_mx(
+                        out=y3[:, u, :],
+                        lhsT=w3_code[half][:, P * n : P * (n + 1)].bitcast(FP8X4),
+                        lhsT_scale=w3_scale[half][:, P * n : P * (n + 1)],
+                        rhs=x_code[c][:].bitcast(FP8X4),
+                        rhs_scale=x_scale[c][:],
+                        start=True,
+                        stop=True,
+                    )
+                y2_out = ring.tile([P, 2, CHUNK], F32, name=f"y2_out{c}_{b}", tag="y2_out", bufs=6)
+                nc.scalar.copy(y2_out[:], y2[:])
+                best = ring.tile([P, 2, CHUNK], F32, name=f"best{c}_{b}", tag="best", bufs=6)
+                nc.vector.tensor_tensor(best[:], y3[:], y2_out[:], ALU.max)
+                nc.sync.dma_start(out_rows[b][:, :, c * CHUNK : (c + 1) * CHUNK], best[:])
+
+        fetch_after(0)
+        for c in range(chunks + 1):
+            if c + 1 < chunks:
+                fetch_after(c + 1)
+            if c < chunks:
+                quantise_x(c)
+            if c > 0:
+                scores(c - 1)

@@ -44,7 +44,7 @@ def tile_list_insulator_patrol_scores_kernel(
             return tile
 
         def load_w1(a):
-            tile = ring.tile([P, PACK, H], F32, name=f"w1_raw{a}", tag="raw", bufs=3)
+            tile = keep.tile([P, PACK, H], F32, name=f"w1_raw{a}")
             rows = w1[a * P * PACK : (a + 1) * P * PACK, :]
             nc.sync.dma_start(tile[:], rows.rearrange("(p j) c -> p j c", j=PACK))
             return tile
@@ -61,23 +61,23 @@ def tile_list_insulator_patrol_scores_kernel(
 
         table_scale = keep.tile([P, T], U8, name="table_scale")
         w2_scale = keep.tile([P, N], U8, name="w2_scale", align_bytes=64)
-        nc.vector.memset(table_scale[:].bitcast(I32), 0)
+        nc.gpsimd.memset(table_scale[:].bitcast(I32), 0)
         nc.vector.memset(w2_scale[:].bitcast(I32), 0)
-        for q in range(4):
-            nc.gpsimd.dma_start(
-                table_scale[32 * q : 32 * q + 4 * PASSES, :].bitcast(I32),
-                tab_scales[:, 4 * q : 4 * q + 4, :].bitcast(I32),
-            )
 
         table, w1_raw, page = {}, {}, {}
         list1 = load_list(offs, "list1")
         table[0] = load_table(0)
-        w1_raw[0] = load_w1(0)
         list4 = load_list(offs4, "list4")
+        w1_raw[0] = load_w1(0)
         page[0] = load_page(0)
+        for q in range(4):
+            nc.sync.dma_start(
+                table_scale[32 * q : 32 * q + 4 * PASSES, :].bitcast(I32),
+                tab_scales[:, 4 * q : 4 * q + 4, :].bitcast(I32),
+            )
         w1_raw[1] = load_w1(1)
-        table[1] = load_table(1)
         w1_raw[2] = load_w1(2)
+        table[1] = load_table(1)
         table[2] = load_table(2)
         bias = load_rows(b1, "bias")
         gains = load_rows(gain, "gains")
@@ -85,7 +85,7 @@ def tile_list_insulator_patrol_scores_kernel(
         page[1] = load_page(1)
         wgs_rows = wgs.rearrange("(q t) j -> q t j", t=PACK)
         factor_first = keep.tile([P, S], F32, name="factor_first")
-        factor_rest = keep.tile([P, PACK - 1, S], F32, name="factor_rest")
+        factor_rest = keep.tile([P, PACK - 1, S], F32, name="factor_rest", align_bytes=64)
         for q in range(4):
             nc.sync.dma_start(factor_first[32 * q : 32 * (q + 1), :], wgs_rows[:, 0, :])
         page[2] = load_page(2)
@@ -105,10 +105,16 @@ def tile_list_insulator_patrol_scores_kernel(
         picked_scale = keep.tile([P, S], U8, name="picked_scale", align_bytes=64)
         w1_code = [keep.tile([P, H], U32, name=f"w1_code{a}", align_bytes=64) for a in range(PASSES)]
         w1_scale = [keep.tile([P, H], U8, name=f"w1_scale{a}", align_bytes=64) for a in range(PASSES)]
-        magnitude = [keep.tile([P, M], F32, name=f"magnitude{t}") for t in range(PACK)]
+        hidden = [keep.tile([P, S], F32, name=f"hidden{t}") for t in range(PACK)]
+        before = [keep.tile([P, M], F32, name=f"before{t}")[:] for t in range(2)] + [hidden[0][:], hidden[1][:]]
+        spent_w1 = w1_raw[PASSES - 1][:].rearrange("p j c -> p (j c)")
+        magnitude = [spent_w1[:, 0:M], factor[0], spent_w1[:, M : 2 * M], before[0]]
 
-        def gather_table(a):
-            nc.vector.tensor_copy(picked[a][:], table[a][:].indirect(list1[:]))
+        def gather_table(a, pieces=1):
+            width = S // pieces
+            for i in range(pieces):
+                offsets = list1[:, i * width // 16 : (i + 1) * width // 16]
+                nc.vector.tensor_copy(picked[a][:, i * width : (i + 1) * width], table[a][:].indirect(offsets))
 
         def quantise_w1(a):
             grouped = ring.tile([P, PACK * H], BF16, name=f"w1_grouped{a}", tag="grouped", align_bytes=64)
@@ -119,31 +125,25 @@ def tile_list_insulator_patrol_scores_kernel(
             nc.vector.quantize_mx(out=w1_code[a][:].bitcast(FP8X4), scales=w1_scale[a][:], in_=grouped[:])
 
         def fetch_before(t):
-            before = ring.tile([P, M], F32, name=f"before{t}", tag="before")
-            nc.vector.tensor_copy(before[:], page[t][:].indirect(list4[:]))
-            nc.scalar.activation(magnitude[t][:], before[:], ACT.Abs)
+            nc.vector.tensor_copy(before[t], page[t][:].indirect(list4[:]))
 
         gather_table(0)
-        nc.vector.tensor_copy(picked_scale[:], table_scale[:].indirect(list1[:]))
         fetch_before(0)
+        nc.vector.tensor_copy(picked_scale[:], table_scale[:].indirect(list1[:]))
         quantise_w1(0)
-        gather_table(1)
         quantise_w1(1)
-        gather_table(2)
+        gather_table(1)
         quantise_w1(2)
+        gather_table(2, pieces=S // BANK)
 
-        hidden = {}
-        for t in range(PACK):
-            if t > 0:
-                fetch_before(t)
-            nc.scalar.activation(factor[t], factor[t], ACT.Copy, scale=gains[:, t : t + 1])
-            hidden[t] = ring.tile([P, S], F32, name=f"hidden{t}", tag="hidden")
-            for half in range(S // BANK):
-                cols = slice(half * BANK, (half + 1) * BANK)
-                acc = psum.tile([P, BANK], F32, name=f"acc{t}_{half}", tag="y2", bufs=4)
-                for a in range(PASSES):
+        def features(t):
+            halves = range(S // BANK)
+            acc = [psum.tile([P, BANK], F32, name=f"acc{t}_{half}", tag="y2", bufs=4) for half in halves]
+            for a in range(PASSES):
+                for half in halves:
+                    cols = slice(half * BANK, (half + 1) * BANK)
                     nc.tensor.matmul_mx(
-                        out=acc[:],
+                        out=acc[half][:],
                         lhsT=w1_code[a][:, t * P : (t + 1) * P].bitcast(FP8X4),
                         lhsT_scale=w1_scale[a][:, t * P : (t + 1) * P],
                         rhs=picked[a][:, cols].bitcast(FP8X4),
@@ -151,40 +151,56 @@ def tile_list_insulator_patrol_scores_kernel(
                         start=(a == 0),
                         stop=(a == PASSES - 1),
                     )
-                nc.scalar.activation(hidden[t][:, cols], acc[:], ACT.Gelu_apprx_tanh, bias=bias[:, t : t + 1])
+            for half in halves:
+                part = hidden[t][:, half * BANK : (half + 1) * BANK]
+                nc.scalar.activation(part, acc[half][:], ACT.Gelu_apprx_tanh, bias=bias[:, t : t + 1])
+                nc.scalar.activation(part, part, ACT.Copy, scale=gains[:, t : t + 1])
+
+        for t in range(PACK):
+            features(t)
+        for t in range(PACK):
+            if t + 1 < PACK:
+                fetch_before(t + 1)
             nc.vector.tensor_tensor(page[t][:].indirect(list2[:]), hidden[t][:], factor[t], ALU.mult)
+        for t in range(PACK):
+            nc.scalar.activation(magnitude[t], before[t], ACT.Abs)
 
         w3_code, w3_scale = [], []
         for u in range(2):
-            raw = ring.tile([P, PACK, W3_HALF], F32, name=f"w3_raw{u}", tag="raw", bufs=3)
+            raw = keep.tile([P, PACK, W3_HALF], F32, name=f"w3_raw{u}")
             nc.sync.dma_start(
                 raw[:], w3[:, u * W3_HALF : (u + 1) * W3_HALF].rearrange("(p j) c -> p j c", j=PACK)
             )
-            grouped = ring.tile([P, PACK * W3_HALF], BF16, name=f"w3_grouped{u}", tag="grouped", align_bytes=64)
-            nc.scalar.copy(grouped[:].rearrange("p (c j) -> p c j", j=PACK), raw[:].rearrange("p j c -> p c j"))
+            grouped = factor[1 + u].bitcast(BF16)[:, 0 : PACK * W3_HALF]
+            nc.scalar.copy(grouped.rearrange("p (c j) -> p c j", j=PACK), raw[:].rearrange("p j c -> p c j"))
             code = keep.tile([P, W3_HALF], U32, name=f"w3_code{u}", align_bytes=64)
             scale = keep.tile([P, W3_HALF], U8, name=f"w3_scale{u}", align_bytes=64)
-            nc.vector.quantize_mx(out=code[:].bitcast(FP8X4), scales=scale[:], in_=grouped[:])
+            nc.vector.quantize_mx(out=code[:].bitcast(FP8X4), scales=scale[:], in_=grouped)
             w3_code.append(code)
             w3_scale.append(scale)
 
         chunks = M // CHUNK
-        diff = [hidden[PACK - 1][:], factor[PACK - 1]]
+        pairs = N // (2 * P)
+        y2_out = [keep.tile([P, pairs * 2 * CHUNK], F32, name=f"y2_out{i}") for i in range(chunks)]
+        last = PACK - 1
+        diff = [hidden[last][:], factor[last], hidden[last][:], y2_out[0][:, 2 * CHUNK : pairs * 2 * CHUNK]]
         out_rows = out.rearrange("(b u p) m -> b p u m", u=2, p=P)
         x_code, x_scale, x_grouped = {}, {}, {}
 
         def fetch_after(c):
             for t in range(PACK):
                 nc.vector.tensor_tensor(
-                    diff[c % 2][:, t * CHUNK : (t + 1) * CHUNK],
+                    diff[c][:, t * CHUNK : (t + 1) * CHUNK],
                     page[t][:].indirect(list3[:, c * CHUNK // 16 : (c + 1) * CHUNK // 16]),
                     magnitude[t][:, c * CHUNK : (c + 1) * CHUNK],
                     ALU.subtract,
                 )
+
+        def group_x(c):
             x_grouped[c] = ring.tile([P, PACK * CHUNK], BF16, name=f"x_grouped{c}", tag="x_grouped", align_bytes=64)
             nc.scalar.copy(
                 x_grouped[c][:].rearrange("p (m t) -> p m t", t=PACK),
-                diff[c % 2].rearrange("p (t m) -> p m t", t=PACK),
+                diff[c].rearrange("p (t m) -> p m t", t=PACK),
             )
 
         def quantise_x(c):
@@ -193,13 +209,13 @@ def tile_list_insulator_patrol_scores_kernel(
             nc.vector.quantize_mx(out=x_code[c][:].bitcast(FP8X4), scales=x_scale[c][:], in_=x_grouped[c][:])
 
         def scores(c):
-            for b in range(N // (2 * P)):
-                y2 = psum.tile([P, 2, CHUNK], F32, name=f"y2_{c}_{b}", tag="y2", bufs=4)
-                y3 = psum.tile([P, 2, CHUNK], F32, name=f"y3_{c}_{b}", tag="y3", bufs=4)
+            for b in range(pairs):
+                y2 = psum.tile([P, 2 * CHUNK], F32, name=f"y2_{c}_{b}", tag="y2", bufs=4)
+                y3 = psum.tile([P, 2 * CHUNK], F32, name=f"y3_{c}_{b}", tag="y3", bufs=4)
                 for u in range(2):
                     n = 2 * b + u
                     nc.tensor.matmul_mx(
-                        out=y2[:, u, :],
+                        out=y2[:, u * CHUNK : (u + 1) * CHUNK],
                         lhsT=w2_code[:, 2 * P * n : 2 * P * (n + 1)].bitcast(FP4X4),
                         lhsT_scale=w2_scale[:, P * n : P * (n + 1)],
                         rhs=x_code[c][:].bitcast(FP8X4),
@@ -210,7 +226,7 @@ def tile_list_insulator_patrol_scores_kernel(
                 for u in range(2):
                     half, n = divmod(2 * b + u, W3_HALF // P)
                     nc.tensor.matmul_mx(
-                        out=y3[:, u, :],
+                        out=y3[:, u * CHUNK : (u + 1) * CHUNK],
                         lhsT=w3_code[half][:, P * n : P * (n + 1)].bitcast(FP8X4),
                         lhsT_scale=w3_scale[half][:, P * n : P * (n + 1)],
                         rhs=x_code[c][:].bitcast(FP8X4),
@@ -218,13 +234,16 @@ def tile_list_insulator_patrol_scores_kernel(
                         start=True,
                         stop=True,
                     )
-                y2_out = ring.tile([P, 2, CHUNK], F32, name=f"y2_out{c}_{b}", tag="y2_out", bufs=6)
-                nc.scalar.copy(y2_out[:], y2[:])
-                best = ring.tile([P, 2, CHUNK], F32, name=f"best{c}_{b}", tag="best", bufs=6)
-                nc.vector.tensor_tensor(best[:], y3[:], y2_out[:], ALU.max)
-                nc.sync.dma_start(out_rows[b][:, :, c * CHUNK : (c + 1) * CHUNK], best[:])
+                kept = y2_out[c][:, b * 2 * CHUNK : (b + 1) * 2 * CHUNK]
+                nc.scalar.copy(kept, y2[:])
+                best = ring.tile([P, 2 * CHUNK], F32, name=f"best{c}_{b}", tag="best", bufs=6)
+                nc.vector.tensor_tensor(best[:], y3[:], kept, ALU.max)
+                nc.sync.dma_start(
+                    out_rows[b][:, :, c * CHUNK : (c + 1) * CHUNK], best[:].rearrange("p (u m) -> p u m", u=2)
+                )
 
         fetch_after(0)
+        group_x(0)
         for c in range(chunks + 1):
             if c + 1 < chunks:
                 fetch_after(c + 1)
@@ -232,3 +251,5 @@ def tile_list_insulator_patrol_scores_kernel(
                 quantise_x(c)
             if c > 0:
                 scores(c - 1)
+            if c + 1 < chunks:
+                group_x(c + 1)

@@ -64,12 +64,25 @@ def tile_list_insulator_patrol_scores_kernel(
         nc.gpsimd.memset(table_scale[:].bitcast(I32), 0)
         nc.vector.memset(w2_scale[:].bitcast(I32), 0)
 
-        table, w1_raw, page = {}, {}, {}
+        def load_factor(t):
+            tile = ring.tile([P, S], F32, name=f"factor{t}", tag=f"factor{t}", bufs=1, align_bytes=64)
+            rows = wgs.rearrange("(q t) j -> t q j", t=PACK)[t]
+            for q in range(4):
+                nc.sync.dma_start(tile[32 * q : 32 * (q + 1), :], rows)
+            return tile
+
+        def load_w3(u):
+            tile = keep.tile([P, PACK, W3_HALF], F32, name=f"w3_raw{u}")
+            cols = w3[:, u * W3_HALF : (u + 1) * W3_HALF]
+            nc.sync.dma_start(tile[:], cols.rearrange("(p j) c -> p j c", j=PACK))
+            return tile
+
+        table, w1_raw, page, factor = {}, {}, {}, {}
         list1 = load_list(offs, "list1")
         table[0] = load_table(0)
         list4 = load_list(offs4, "list4")
-        w1_raw[0] = load_w1(0)
         page[0] = load_page(0)
+        w1_raw[0] = load_w1(0)
         for q in range(4):
             nc.sync.dma_start(
                 table_scale[32 * q : 32 * q + 4 * PASSES, :].bitcast(I32),
@@ -83,16 +96,13 @@ def tile_list_insulator_patrol_scores_kernel(
         gains = load_rows(gain, "gains")
         list2 = load_list(offs2, "list2")
         page[1] = load_page(1)
-        wgs_rows = wgs.rearrange("(q t) j -> q t j", t=PACK)
-        factor_first = keep.tile([P, S], F32, name="factor_first")
-        factor_rest = keep.tile([P, PACK - 1, S], F32, name="factor_rest", align_bytes=64)
-        for q in range(4):
-            nc.sync.dma_start(factor_first[32 * q : 32 * (q + 1), :], wgs_rows[:, 0, :])
+        factor[0] = load_factor(0)
         page[2] = load_page(2)
-        for q in range(4):
-            nc.sync.dma_start(factor_rest[32 * q : 32 * (q + 1), :, :], wgs_rows[:, 1:PACK, :])
+        factor[1] = load_factor(1)
         page[3] = load_page(3)
-        factor = [factor_first[:]] + [factor_rest[:, t, :] for t in range(PACK - 1)]
+        factor[2] = load_factor(2)
+        w3_raw = [load_w3(u) for u in range(2)]
+        factor[3] = load_factor(3)
         list3 = load_list(offs3, "list3")
         w2_code = keep.tile([P, 2 * N], U8, name="w2_code", align_bytes=64)
         nc.sync.dma_start(w2_code[:].bitcast(I32), w2_words[0].bitcast(I32))
@@ -103,12 +113,15 @@ def tile_list_insulator_patrol_scores_kernel(
 
         picked = [keep.tile([P, S], U32, name=f"picked{a}", align_bytes=64) for a in range(PASSES)]
         picked_scale = keep.tile([P, S], U8, name="picked_scale", align_bytes=64)
-        w1_code = [keep.tile([P, H], U32, name=f"w1_code{a}", align_bytes=64) for a in range(PASSES)]
-        w1_scale = [keep.tile([P, H], U8, name=f"w1_scale{a}", align_bytes=64) for a in range(PASSES)]
-        hidden = [keep.tile([P, S], F32, name=f"hidden{t}") for t in range(PACK)]
+        hidden = [keep.tile([P, S], F32, name=f"hidden{t}", align_bytes=64) for t in range(PACK)]
+        early = keep.tile([P, 2 * S], F32, name="early", align_bytes=64)
+        activated = [early[:, 0:S], early[:, S : 2 * S], hidden[2][:], hidden[3][:]]
+        first_pair = keep.tile([P, 2 * K], BF16, name="first_pair", align_bytes=64)
+        w1_grouped = [first_pair[:], early[:].bitcast(BF16)[:, 0 : 2 * K]]
         before = [keep.tile([P, M], F32, name=f"before{t}")[:] for t in range(2)] + [hidden[0][:], hidden[1][:]]
         spent_w1 = w1_raw[PASSES - 1][:].rearrange("p j c -> p (j c)")
-        magnitude = [spent_w1[:, 0:M], factor[0], spent_w1[:, M : 2 * M], before[0]]
+        magnitude = [spent_w1[:, 0:M], early[:, 0:M], spent_w1[:, M : 2 * M], before[0]]
+        w1_code, w1_scale = {}, {}
 
         def gather_table(a, pieces=1):
             width = S // pieces
@@ -116,25 +129,27 @@ def tile_list_insulator_patrol_scores_kernel(
                 offsets = list1[:, i * width // 16 : (i + 1) * width // 16]
                 nc.vector.tensor_copy(picked[a][:, i * width : (i + 1) * width], table[a][:].indirect(offsets))
 
-        def quantise_w1(a):
-            grouped = ring.tile([P, PACK * H], BF16, name=f"w1_grouped{a}", tag="grouped", align_bytes=64)
+        def group_w1(pair, a):
             nc.scalar.copy(
-                grouped[:].rearrange("p (t m j) -> p m t j", t=PACK, j=PACK),
-                w1_raw[a][:].rearrange("p j (m t) -> p m t j", t=PACK),
+                w1_grouped[pair].rearrange("p (t a m j) -> p a m j t", t=2, a=PASSES, j=PACK)[:, a],
+                w1_raw[a][:].rearrange("p j (m u t) -> p u m j t", u=2, t=2)[:, pair],
             )
-            nc.vector.quantize_mx(out=w1_code[a][:].bitcast(FP8X4), scales=w1_scale[a][:], in_=grouped[:])
+
+        def quantise_w1(t):
+            if t < 2:
+                w1_code[t] = keep.tile([P, K // PACK], U32, name=f"w1_code{t}", align_bytes=64)
+            else:
+                tag = f"factor{t - 2}"
+                w1_code[t] = ring.tile([P, K // PACK], U32, name=f"w1_code{t}", tag=tag, bufs=1, align_bytes=64)
+            w1_scale[t] = keep.tile([P, K // PACK], U8, name=f"w1_scale{t}", align_bytes=64)
+            nc.vector.quantize_mx(
+                out=w1_code[t][:].bitcast(FP8X4),
+                scales=w1_scale[t][:],
+                in_=w1_grouped[t // 2][:, (t % 2) * K : (t % 2 + 1) * K],
+            )
 
         def fetch_before(t):
             nc.vector.tensor_copy(before[t], page[t][:].indirect(list4[:]))
-
-        gather_table(0)
-        fetch_before(0)
-        nc.vector.tensor_copy(picked_scale[:], table_scale[:].indirect(list1[:]))
-        quantise_w1(0)
-        quantise_w1(1)
-        gather_table(1)
-        quantise_w1(2)
-        gather_table(2, pieces=S // BANK)
 
         def features(t):
             halves = range(S // BANK)
@@ -144,36 +159,56 @@ def tile_list_insulator_patrol_scores_kernel(
                     cols = slice(half * BANK, (half + 1) * BANK)
                     nc.tensor.matmul_mx(
                         out=acc[half][:],
-                        lhsT=w1_code[a][:, t * P : (t + 1) * P].bitcast(FP8X4),
-                        lhsT_scale=w1_scale[a][:, t * P : (t + 1) * P],
+                        lhsT=w1_code[t][:, a * P : (a + 1) * P].bitcast(FP8X4),
+                        lhsT_scale=w1_scale[t][:, a * P : (a + 1) * P],
                         rhs=picked[a][:, cols].bitcast(FP8X4),
                         rhs_scale=picked_scale[4 * a : P, cols],
                         start=(a == 0),
                         stop=(a == PASSES - 1),
                     )
             for half in halves:
-                part = hidden[t][:, half * BANK : (half + 1) * BANK]
+                cols = slice(half * BANK, (half + 1) * BANK)
+                part = activated[t][:, cols]
                 nc.scalar.activation(part, acc[half][:], ACT.Gelu_apprx_tanh, bias=bias[:, t : t + 1])
-                nc.scalar.activation(part, part, ACT.Copy, scale=gains[:, t : t + 1])
+                nc.scalar.activation(hidden[t][:, cols], part, ACT.Copy, scale=gains[:, t : t + 1])
 
+        def rewrite_page(t):
+            nc.vector.tensor_tensor(page[t][:].indirect(list2[:]), hidden[t][:], factor[t][:], ALU.mult)
+
+        gather_table(0)
+        fetch_before(0)
+        nc.vector.tensor_copy(picked_scale[:], table_scale[:].indirect(list1[:]))
+        for a in range(PASSES):
+            group_w1(0, a)
+        quantise_w1(0)
+        quantise_w1(1)
+        gather_table(1)
+        gather_table(2, pieces=S // BANK)
+        features(0)
+        features(1)
+        for a in range(PASSES):
+            group_w1(1, a)
+        fetch_before(1)
         for t in range(PACK):
-            features(t)
-        for t in range(PACK):
-            if t + 1 < PACK:
-                fetch_before(t + 1)
-            nc.vector.tensor_tensor(page[t][:].indirect(list2[:]), hidden[t][:], factor[t], ALU.mult)
+            rewrite_page(t)
+            if t + 2 < PACK:
+                fetch_before(t + 2)
+                quantise_w1(t + 2)
+                features(t + 2)
         for t in range(PACK):
             nc.scalar.activation(magnitude[t], before[t], ACT.Abs)
 
+        def interleave(grouped, rows):
+            nc.scalar.copy(
+                grouped.rearrange("p (c i j) -> p c j i", i=4, j=PACK),
+                rows.rearrange("p j (c i) -> p c j i", i=4),
+            )
+
         w3_code, w3_scale = [], []
         for u in range(2):
-            raw = keep.tile([P, PACK, W3_HALF], F32, name=f"w3_raw{u}")
-            nc.sync.dma_start(
-                raw[:], w3[:, u * W3_HALF : (u + 1) * W3_HALF].rearrange("(p j) c -> p j c", j=PACK)
-            )
-            grouped = factor[1 + u].bitcast(BF16)[:, 0 : PACK * W3_HALF]
-            nc.scalar.copy(grouped.rearrange("p (c j) -> p c j", j=PACK), raw[:].rearrange("p j c -> p c j"))
-            code = keep.tile([P, W3_HALF], U32, name=f"w3_code{u}", align_bytes=64)
+            grouped = first_pair[:, u * PACK * W3_HALF : (u + 1) * PACK * W3_HALF]
+            interleave(grouped, w3_raw[u][:])
+            code = ring.tile([P, W3_HALF], U32, name=f"w3_code{u}", tag=f"factor{u}", bufs=1, align_bytes=64)
             scale = keep.tile([P, W3_HALF], U8, name=f"w3_scale{u}", align_bytes=64)
             nc.vector.quantize_mx(out=code[:].bitcast(FP8X4), scales=scale[:], in_=grouped)
             w3_code.append(code)
@@ -183,7 +218,7 @@ def tile_list_insulator_patrol_scores_kernel(
         pairs = N // (2 * P)
         y2_out = [keep.tile([P, pairs * 2 * CHUNK], F32, name=f"y2_out{i}") for i in range(chunks)]
         last = PACK - 1
-        diff = [hidden[last][:], factor[last], hidden[last][:], y2_out[0][:, 2 * CHUNK : pairs * 2 * CHUNK]]
+        diff = [hidden[last][:], factor[last][:], hidden[last][:], y2_out[0][:, 2 * CHUNK : pairs * 2 * CHUNK]]
         out_rows = out.rearrange("(b u p) m -> b p u m", u=2, p=P)
         x_code, x_scale, x_grouped = {}, {}, {}
 
@@ -198,10 +233,7 @@ def tile_list_insulator_patrol_scores_kernel(
 
         def group_x(c):
             x_grouped[c] = ring.tile([P, PACK * CHUNK], BF16, name=f"x_grouped{c}", tag="x_grouped", align_bytes=64)
-            nc.scalar.copy(
-                x_grouped[c][:].rearrange("p (m t) -> p m t", t=PACK),
-                diff[c].rearrange("p (t m) -> p m t", t=PACK),
-            )
+            interleave(x_grouped[c][:], diff[c].rearrange("p (t m) -> p t m", t=PACK))
 
         def quantise_x(c):
             x_code[c] = ring.tile([P, CHUNK], U32, name=f"x_code{c}", tag="x_code", align_bytes=64)

@@ -20,7 +20,8 @@ P = 128
 PACK = 4
 PASSES = K // (P * PACK)
 BANK = 512
-CHUNK = 256
+CHUNKS = (512, 256, 256)
+LEAD = 256
 W3_HALF = N // 2
 
 
@@ -65,9 +66,12 @@ def tile_list_insulator_patrol_scores_kernel(
         nc.vector.memset(w2_scale[:].bitcast(I32), 0)
 
         def load_factor(t):
-            tile = ring.tile([P, S], F32, name=f"factor{t}", tag=f"factor{t}", bufs=1, align_bytes=64)
+            if t < PACK - 1:
+                tile = ring.tile([P, S], F32, name=f"factor{t}", tag=f"factor{t}", bufs=1, align_bytes=64)[:]
+            else:
+                tile = closing[:, LEAD + S : LEAD + 2 * S]
             rows = wgs.rearrange("(q t) j -> t q j", t=PACK)[t]
-            for q in range(4):
+            for q in (0, 2, 1, 3):
                 nc.sync.dma_start(tile[32 * q : 32 * (q + 1), :], rows)
             return tile
 
@@ -77,13 +81,14 @@ def tile_list_insulator_patrol_scores_kernel(
             nc.sync.dma_start(tile[:], cols.rearrange("(p j) c -> p j c", j=PACK))
             return tile
 
+        closing = keep.tile([P, PACK * (CHUNKS[0] + CHUNKS[1])], F32, name="closing")
         table, w1_raw, page, factor = {}, {}, {}, {}
         list1 = load_list(offs, "list1")
         table[0] = load_table(0)
         list4 = load_list(offs4, "list4")
         page[0] = load_page(0)
         w1_raw[0] = load_w1(0)
-        for q in range(4):
+        for q in (0, 2, 1, 3):
             nc.sync.dma_start(
                 table_scale[32 * q : 32 * q + 4 * PASSES, :].bitcast(I32),
                 tab_scales[:, 4 * q : 4 * q + 4, :].bitcast(I32),
@@ -113,12 +118,13 @@ def tile_list_insulator_patrol_scores_kernel(
 
         picked = [keep.tile([P, S], U32, name=f"picked{a}", align_bytes=64) for a in range(PASSES)]
         picked_scale = keep.tile([P, S], U8, name="picked_scale", align_bytes=64)
-        hidden = [keep.tile([P, S], F32, name=f"hidden{t}", align_bytes=64) for t in range(PACK)]
+        hidden = [keep.tile([P, S], F32, name=f"hidden{t}")[:] for t in range(PACK - 1)]
+        hidden.append(closing[:, LEAD : LEAD + S])
         early = keep.tile([P, 2 * S], F32, name="early", align_bytes=64)
-        activated = [early[:, 0:S], early[:, S : 2 * S], hidden[2][:], hidden[3][:]]
+        activated = [early[:, 0:S], early[:, S : 2 * S], hidden[2], hidden[3]]
         first_pair = keep.tile([P, 2 * K], BF16, name="first_pair", align_bytes=64)
         w1_grouped = [first_pair[:], early[:].bitcast(BF16)[:, 0 : 2 * K]]
-        before = [keep.tile([P, M], F32, name=f"before{t}")[:] for t in range(2)] + [hidden[0][:], hidden[1][:]]
+        before = [keep.tile([P, M], F32, name=f"before{t}")[:] for t in range(2)] + [hidden[0], hidden[1]]
         spent_w1 = w1_raw[PASSES - 1][:].rearrange("p j c -> p (j c)")
         magnitude = [spent_w1[:, 0:M], early[:, 0:M], spent_w1[:, M : 2 * M], before[0]]
         w1_code, w1_scale = {}, {}
@@ -154,18 +160,21 @@ def tile_list_insulator_patrol_scores_kernel(
         def features(t):
             halves = range(S // BANK)
             acc = [psum.tile([P, BANK], F32, name=f"acc{t}_{half}", tag="y2", bufs=4) for half in halves]
-            for a in range(PASSES):
-                for half in halves:
-                    cols = slice(half * BANK, (half + 1) * BANK)
-                    nc.tensor.matmul_mx(
-                        out=acc[half][:],
-                        lhsT=w1_code[t][:, a * P : (a + 1) * P].bitcast(FP8X4),
-                        lhsT_scale=w1_scale[t][:, a * P : (a + 1) * P],
-                        rhs=picked[a][:, cols].bitcast(FP8X4),
-                        rhs_scale=picked_scale[4 * a : P, cols],
-                        start=(a == 0),
-                        stop=(a == PASSES - 1),
-                    )
+            if t == 0:
+                steps = [(a, half) for a in range(PASSES) for half in halves]
+            else:
+                steps = [(a, half) for half in halves for a in range(PASSES)]
+            for a, half in steps:
+                cols = slice(half * BANK, (half + 1) * BANK)
+                nc.tensor.matmul_mx(
+                    out=acc[half][:],
+                    lhsT=w1_code[t][:, a * P : (a + 1) * P].bitcast(FP8X4),
+                    lhsT_scale=w1_scale[t][:, a * P : (a + 1) * P],
+                    rhs=picked[a][:, cols].bitcast(FP8X4),
+                    rhs_scale=picked_scale[4 * a : P, cols],
+                    start=(a == 0),
+                    stop=(a == PASSES - 1),
+                )
             for half in halves:
                 cols = slice(half * BANK, (half + 1) * BANK)
                 part = activated[t][:, cols]
@@ -173,7 +182,7 @@ def tile_list_insulator_patrol_scores_kernel(
                 nc.scalar.activation(hidden[t][:, cols], part, ACT.Copy, scale=gains[:, t : t + 1])
 
         def rewrite_page(t):
-            nc.vector.tensor_tensor(page[t][:].indirect(list2[:]), hidden[t][:], factor[t][:], ALU.mult)
+            nc.vector.tensor_tensor(page[t][:].indirect(list2[:]), hidden[t], factor[t], ALU.mult)
 
         gather_table(0)
         fetch_before(0)
@@ -214,40 +223,46 @@ def tile_list_insulator_patrol_scores_kernel(
             w3_code.append(code)
             w3_scale.append(scale)
 
-        chunks = M // CHUNK
-        pairs = N // (2 * P)
-        y2_out = [keep.tile([P, pairs * 2 * CHUNK], F32, name=f"y2_out{i}") for i in range(chunks)]
-        last = PACK - 1
-        diff = [hidden[last][:], factor[last][:], hidden[last][:], y2_out[0][:, 2 * CHUNK : pairs * 2 * CHUNK]]
-        out_rows = out.rearrange("(b u p) m -> b p u m", u=2, p=P)
-        x_code, x_scale, x_grouped = {}, {}, {}
+        starts = [sum(CHUNKS[:c]) for c in range(len(CHUNKS))]
+        closing_rows = closing[:].rearrange("p (t m) -> p t m", t=PACK)
+        diff, x_code, x_scale, x_grouped = {}, {}, {}, {}
 
         def fetch_after(c):
+            first, width = starts[c], CHUNKS[c]
+            if c < 2:
+                diff[c] = closing_rows[:, :, first : first + width]
+            else:
+                diff[c] = ring.tile([P, PACK, width], F32, name=f"diff{c}", tag="x_grouped0", bufs=1, align_bytes=64)
             for t in range(PACK):
                 nc.vector.tensor_tensor(
-                    diff[c][:, t * CHUNK : (t + 1) * CHUNK],
-                    page[t][:].indirect(list3[:, c * CHUNK // 16 : (c + 1) * CHUNK // 16]),
-                    magnitude[t][:, c * CHUNK : (c + 1) * CHUNK],
+                    diff[c][:, t, :],
+                    page[t][:].indirect(list3[:, first // 16 : (first + width) // 16]),
+                    magnitude[t][:, first : first + width],
                     ALU.subtract,
                 )
 
         def group_x(c):
-            x_grouped[c] = ring.tile([P, PACK * CHUNK], BF16, name=f"x_grouped{c}", tag="x_grouped", align_bytes=64)
-            interleave(x_grouped[c][:], diff[c].rearrange("p (t m) -> p t m", t=PACK))
+            x_grouped[c] = ring.tile(
+                [P, PACK * CHUNKS[c]], BF16, name=f"x_grouped{c}", tag=f"x_grouped{c}", bufs=1, align_bytes=64
+            )
+            interleave(x_grouped[c][:], diff[c][:, :, :])
 
         def quantise_x(c):
-            x_code[c] = ring.tile([P, CHUNK], U32, name=f"x_code{c}", tag="x_code", align_bytes=64)
-            x_scale[c] = ring.tile([P, CHUNK], U8, name=f"x_scale{c}", tag="x_scale", align_bytes=64)
+            x_code[c] = keep.tile([P, CHUNKS[c]], U32, name=f"x_code{c}", align_bytes=64)
+            x_scale[c] = keep.tile([P, CHUNKS[c]], U8, name=f"x_scale{c}", align_bytes=64)
             nc.vector.quantize_mx(out=x_code[c][:].bitcast(FP8X4), scales=x_scale[c][:], in_=x_grouped[c][:])
 
         def scores(c):
-            for b in range(pairs):
-                y2 = psum.tile([P, 2 * CHUNK], F32, name=f"y2_{c}_{b}", tag="y2", bufs=4)
-                y3 = psum.tile([P, 2 * CHUNK], F32, name=f"y3_{c}_{b}", tag="y3", bufs=4)
-                for u in range(2):
-                    n = 2 * b + u
+            first, width = starts[c], CHUNKS[c]
+            share = BANK // width
+            out_rows = out.rearrange("(b u p) m -> b p u m", u=share, p=P)
+            for b in range(N // (share * P)):
+                y2 = psum.tile([P, BANK], F32, name=f"y2_{c}_{b}", tag="y2", bufs=4)
+                y3 = psum.tile([P, BANK], F32, name=f"y3_{c}_{b}", tag="y3", bufs=4)
+                for u in range(share):
+                    n = share * b + u
                     nc.tensor.matmul_mx(
-                        out=y2[:, u * CHUNK : (u + 1) * CHUNK],
+                        out=y2[:, u * width : (u + 1) * width],
                         lhsT=w2_code[:, 2 * P * n : 2 * P * (n + 1)].bitcast(FP4X4),
                         lhsT_scale=w2_scale[:, P * n : P * (n + 1)],
                         rhs=x_code[c][:].bitcast(FP8X4),
@@ -255,10 +270,10 @@ def tile_list_insulator_patrol_scores_kernel(
                         start=True,
                         stop=True,
                     )
-                for u in range(2):
-                    half, n = divmod(2 * b + u, W3_HALF // P)
+                for u in range(share):
+                    half, n = divmod(share * b + u, W3_HALF // P)
                     nc.tensor.matmul_mx(
-                        out=y3[:, u * CHUNK : (u + 1) * CHUNK],
+                        out=y3[:, u * width : (u + 1) * width],
                         lhsT=w3_code[half][:, P * n : P * (n + 1)].bitcast(FP8X4),
                         lhsT_scale=w3_scale[half][:, P * n : P * (n + 1)],
                         rhs=x_code[c][:].bitcast(FP8X4),
@@ -266,22 +281,22 @@ def tile_list_insulator_patrol_scores_kernel(
                         start=True,
                         stop=True,
                     )
-                kept = y2_out[c][:, b * 2 * CHUNK : (b + 1) * 2 * CHUNK]
-                nc.scalar.copy(kept, y2[:])
-                best = ring.tile([P, 2 * CHUNK], F32, name=f"best{c}_{b}", tag="best", bufs=6)
-                nc.vector.tensor_tensor(best[:], y3[:], kept, ALU.max)
+                kept = ring.tile([P, BANK], F32, name=f"kept{c}_{b}", tag="kept", bufs=8)
+                nc.scalar.copy(kept[:], y2[:])
+                best = ring.tile([P, BANK], F32, name=f"best{c}_{b}", tag="best", bufs=6)
+                nc.vector.tensor_tensor(best[:], y3[:], kept[:], ALU.max)
                 nc.sync.dma_start(
-                    out_rows[b][:, :, c * CHUNK : (c + 1) * CHUNK], best[:].rearrange("p (u m) -> p u m", u=2)
+                    out_rows[b][:, :, first : first + width], best[:].rearrange("p (u m) -> p u m", u=share)
                 )
 
         fetch_after(0)
         group_x(0)
-        for c in range(chunks + 1):
-            if c + 1 < chunks:
+        for c in range(len(CHUNKS) + 1):
+            if c + 1 < len(CHUNKS):
                 fetch_after(c + 1)
-            if c < chunks:
+            if c < len(CHUNKS):
                 quantise_x(c)
             if c > 0:
                 scores(c - 1)
-            if c + 1 < chunks:
+            if c + 1 < len(CHUNKS):
                 group_x(c + 1)

from contextlib import ExitStack

import concourse.mybir as mybir

K, T, S, H, T2, M, N = 1536, 2048, 1024, 512, 2048, 1024, 768
FLOPS = 2 * K * H * S + 2 * 2 * H * N * M

F32 = mybir.dt.float32
BF16 = mybir.dt.bfloat16
I32 = mybir.dt.int32
U32 = mybir.dt.uint32
U16 = mybir.dt.uint16
U8 = mybir.dt.uint8
FP8X4 = mybir.dt.float8_e4m3fn_x4
FP4X4 = mybir.dt.float4_e2m1fn_x4
ACT = mybir.ActivationFunctionType
ALU = mybir.AluOpType

P = 128
PACK = 4
PASSES = K // (P * PACK)
BANK = 512
CHUNKS = (512, 256, 256)
LEAD = 256
W3_HALF = N // 2


def tile_list_insulator_patrol_scores_kernel(
    tc, tab_words, tab_scales, offs, offs2, offs3, offs4, w1, b1, gain, wgs, page0, w2_words, w2_scales, w3, out
):
    nc = tc.nc
    with ExitStack() as ctx:
        keep = ctx.enter_context(tc.tile_pool(name="keep", bufs=1))
        ring = ctx.enter_context(tc.tile_pool(name="ring", bufs=2))
        psum = ctx.enter_context(tc.psum_pool(name="psum", bufs=1))

        def load_list(src, name):
            tile = keep.tile([P, src.shape[1]], U16, name=name)
            nc.sync.dma_start(tile[:], src)
            return tile

        def load_table(a):
            tile = keep.tile([P, T], U32, name=f"table{a}")
            nc.sync.dma_start(tile[:].bitcast(I32), tab_words[a].rearrange("p t i -> p (t i)").bitcast(I32))
            return tile

        def load_w1(a):
            tile = keep.tile([P, PACK, H], F32, name=f"w1_raw{a}")
            rows = w1[a * P * PACK : (a + 1) * P * PACK, :]
            nc.sync.dma_start(tile[:], rows.rearrange("(p j) c -> p j c", j=PACK))
            return tile

        def load_page(t):
            tile = keep.tile([P, T2], F32, name=f"page{t}")
            nc.sync.dma_start(tile[:], page0.rearrange("(p t) c -> t p c", t=PACK)[t])
            return tile

        def load_rows(src, name):
            tile = keep.tile([P, PACK], F32, name=name)
            nc.sync.dma_start(tile[:], src.rearrange("(p t) -> p t", t=PACK))
            return tile

        table_scale = keep.tile([P, T], U8, name="table_scale")
        w2_scale = keep.tile([P, N], U8, name="w2_scale", align_bytes=64)
        nc.gpsimd.memset(table_scale[:].bitcast(I32), 0)
        nc.vector.memset(w2_scale[:].bitcast(I32), 0)

        def load_factor(t):
            if t < PACK - 1:
                tile = ring.tile([P, S], F32, name=f"factor{t}", tag=f"factor{t}", bufs=1, align_bytes=64)[:]
            else:
                tile = closing[:, LEAD + S : LEAD + 2 * S]
            rows = wgs.rearrange("(q t) j -> t q j", t=PACK)[t]
            for q in (0, 2, 1, 3):
                nc.sync.dma_start(tile[32 * q : 32 * (q + 1), :], rows)
            return tile

        def load_w3(u):
            tile = keep.tile([P, PACK, W3_HALF], F32, name=f"w3_raw{u}")
            cols = w3[:, u * W3_HALF : (u + 1) * W3_HALF]
            nc.sync.dma_start(tile[:], cols.rearrange("(p j) c -> p j c", j=PACK))
            return tile

        closing = keep.tile([P, PACK * (CHUNKS[0] + CHUNKS[1])], F32, name="closing")
        table, w1_raw, page, factor = {}, {}, {}, {}
        list1 = load_list(offs, "list1")
        table[0] = load_table(0)
        list4 = load_list(offs4, "list4")
        page[0] = load_page(0)
        w1_raw[0] = load_w1(0)
        for q in (0, 2, 1, 3):
            nc.sync.dma_start(
                table_scale[32 * q : 32 * q + 4 * PASSES, :].bitcast(I32),
                tab_scales[:, 4 * q : 4 * q + 4, :].bitcast(I32),
            )
        w1_raw[1] = load_w1(1)
        w1_raw[2] = load_w1(2)
        table[1] = load_table(1)
        table[2] = load_table(2)
        bias = load_rows(b1, "bias")
        gains = load_rows(gain, "gains")
        list2 = load_list(offs2, "list2")
        page[1] = load_page(1)
        factor[0] = load_factor(0)
        page[2] = load_page(2)
        factor[1] = load_factor(1)
        page[3] = load_page(3)
        factor[2] = load_factor(2)
        w3_raw = [load_w3(u) for u in range(2)]
        factor[3] = load_factor(3)
        list3 = load_list(offs3, "list3")
        w2_code = keep.tile([P, 2 * N], U8, name="w2_code", align_bytes=64)
        nc.sync.dma_start(w2_code[:].bitcast(I32), w2_words[0].bitcast(I32))
        for q in range(4):
            nc.sync.dma_start(
                w2_scale[32 * q : 32 * q + 4, :].bitcast(I32), w2_scales[0, 4 * q : 4 * q + 4, :].bitcast(I32)
            )

        picked = [keep.tile([P, S], U32, name=f"picked{a}", align_bytes=64) for a in range(PASSES)]
        picked_scale = keep.tile([P, S], U8, name="picked_scale", align_bytes=64)
        hidden = [keep.tile([P, S], F32, name=f"hidden{t}")[:] for t in range(PACK - 1)]
        hidden.append(closing[:, LEAD : LEAD + S])
        early = keep.tile([P, 2 * S], F32, name="early", align_bytes=64)
        activated = [early[:, 0:S], early[:, S : 2 * S], hidden[2], hidden[3]]
        first_pair = keep.tile([P, 2 * K], BF16, name="first_pair", align_bytes=64)
        w1_grouped = [first_pair[:], early[:].bitcast(BF16)[:, 0 : 2 * K]]
        before = [keep.tile([P, M], F32, name=f"before{t}")[:] for t in range(2)] + [hidden[0], hidden[1]]
        spent_w1 = w1_raw[PASSES - 1][:].rearrange("p j c -> p (j c)")
        magnitude = [spent_w1[:, 0:M], early[:, 0:M], spent_w1[:, M : 2 * M], before[0]]
        w1_code, w1_scale = {}, {}

        def gather_table(a, pieces=1):
            width = S // pieces
            for i in range(pieces):
                offsets = list1[:, i * width // 16 : (i + 1) * width // 16]
                nc.vector.tensor_copy(picked[a][:, i * width : (i + 1) * width], table[a][:].indirect(offsets))

        def group_w1(pair, a):
            nc.scalar.copy(
                w1_grouped[pair].rearrange("p (t a m j) -> p a m j t", t=2, a=PASSES, j=PACK)[:, a],
                w1_raw[a][:].rearrange("p j (m u t) -> p u m j t", u=2, t=2)[:, pair],
            )

        def quantise_w1(t):
            if t < 2:
                w1_code[t] = keep.tile([P, K // PACK], U32, name=f"w1_code{t}", align_bytes=64)
            else:
                tag = f"factor{t - 2}"
                w1_code[t] = ring.tile([P, K // PACK], U32, name=f"w1_code{t}", tag=tag, bufs=1, align_bytes=64)
            w1_scale[t] = keep.tile([P, K // PACK], U8, name=f"w1_scale{t}", align_bytes=64)
            nc.vector.quantize_mx(
                out=w1_code[t][:].bitcast(FP8X4),
                scales=w1_scale[t][:],
                in_=w1_grouped[t // 2][:, (t % 2) * K : (t % 2 + 1) * K],
            )

        def fetch_before(t):
            nc.vector.tensor_copy(before[t], page[t][:].indirect(list4[:]))

        def features(t):
            halves = range(S // BANK)
            acc = [psum.tile([P, BANK], F32, name=f"acc{t}_{half}", tag="y2", bufs=4) for half in halves]
            if t == 0:
                steps = [(a, half) for a in range(PASSES) for half in halves]
            else:
                steps = [(a, half) for half in halves for a in range(PASSES)]
            for a, half in steps:
                cols = slice(half * BANK, (half + 1) * BANK)
                nc.tensor.matmul_mx(
                    out=acc[half][:],
                    lhsT=w1_code[t][:, a * P : (a + 1) * P].bitcast(FP8X4),
                    lhsT_scale=w1_scale[t][:, a * P : (a + 1) * P],
                    rhs=picked[a][:, cols].bitcast(FP8X4),
                    rhs_scale=picked_scale[4 * a : P, cols],
                    start=(a == 0),
                    stop=(a == PASSES - 1),
                )
            for half in halves:
                cols = slice(half * BANK, (half + 1) * BANK)
                part = activated[t][:, cols]
                nc.scalar.activation(part, acc[half][:], ACT.Gelu_apprx_tanh, bias=bias[:, t : t + 1])
                nc.scalar.activation(hidden[t][:, cols], part, ACT.Copy, scale=gains[:, t : t + 1])

        def rewrite_page(t):
            nc.vector.tensor_tensor(page[t][:].indirect(list2[:]), hidden[t], factor[t], ALU.mult)

        gather_table(0)
        fetch_before(0)
        nc.vector.tensor_copy(picked_scale[:], table_scale[:].indirect(list1[:]))
        for a in range(PASSES):
            group_w1(0, a)
        quantise_w1(0)
        quantise_w1(1)
        gather_table(1)
        gather_table(2, pieces=S // BANK)
        features(0)
        features(1)
        for a in range(PASSES):
            group_w1(1, a)
        fetch_before(1)
        for t in range(PACK):
            rewrite_page(t)
            if t + 2 < PACK:
                fetch_before(t + 2)
                quantise_w1(t + 2)
                features(t + 2)
        for t in range(PACK):
            nc.scalar.activation(magnitude[t], before[t], ACT.Abs)

        def interleave(grouped, rows):
            nc.scalar.copy(
                grouped.rearrange("p (c i j) -> p c j i", i=4, j=PACK),
                rows.rearrange("p j (c i) -> p c j i", i=4),
            )

        w3_code, w3_scale = [], []
        for u in range(2):
            grouped = first_pair[:, u * PACK * W3_HALF : (u + 1) * PACK * W3_HALF]
            interleave(grouped, w3_raw[u][:])
            code = ring.tile([P, W3_HALF], U32, name=f"w3_code{u}", tag=f"factor{u}", bufs=1, align_bytes=64)
            scale = keep.tile([P, W3_HALF], U8, name=f"w3_scale{u}", align_bytes=64)
            nc.vector.quantize_mx(out=code[:].bitcast(FP8X4), scales=scale[:], in_=grouped)
            w3_code.append(code)
            w3_scale.append(scale)

        starts = [sum(CHUNKS[:c]) for c in range(len(CHUNKS))]
        closing_rows = closing[:].rearrange("p (t m) -> p t m", t=PACK)
        diff, x_code, x_scale, x_grouped = {}, {}, {}, {}

        def fetch_after(c):
            first, width = starts[c], CHUNKS[c]
            if c < 2:
                diff[c] = closing_rows[:, :, first : first + width]
            else:
                diff[c] = ring.tile([P, PACK, width], F32, name=f"diff{c}", tag="x_grouped0", bufs=1, align_bytes=64)
            for t in range(PACK):
                nc.vector.tensor_tensor(
                    diff[c][:, t, :],
                    page[t][:].indirect(list3[:, first // 16 : (first + width) // 16]),
                    magnitude[t][:, first : first + width],
                    ALU.subtract,
                )

        def group_x(c):
            x_grouped[c] = ring.tile(
                [P, PACK * CHUNKS[c]], BF16, name=f"x_grouped{c}", tag=f"x_grouped{c}", bufs=1, align_bytes=64
            )
            interleave(x_grouped[c][:], diff[c][:, :, :])

        def quantise_x(c):
            x_code[c] = keep.tile([P, CHUNKS[c]], U32, name=f"x_code{c}", align_bytes=64)
            x_scale[c] = keep.tile([P, CHUNKS[c]], U8, name=f"x_scale{c}", align_bytes=64)
            nc.vector.quantize_mx(out=x_code[c][:].bitcast(FP8X4), scales=x_scale[c][:], in_=x_grouped[c][:])

        def scores(c):
            first, width = starts[c], CHUNKS[c]
            share = BANK // width
            out_rows = out.rearrange("(b u p) m -> b p u m", u=share, p=P)
            for b in range(N // (share * P)):
                y2 = psum.tile([P, BANK], F32, name=f"y2_{c}_{b}", tag="y2", bufs=4)
                y3 = psum.tile([P, BANK], F32, name=f"y3_{c}_{b}", tag="y3", bufs=4)
                for u in range(share):
                    n = share * b + u
                    nc.tensor.matmul_mx(
                        out=y2[:, u * width : (u + 1) * width],
                        lhsT=w2_code[:, 2 * P * n : 2 * P * (n + 1)].bitcast(FP4X4),
                        lhsT_scale=w2_scale[:, P * n : P * (n + 1)],
                        rhs=x_code[c][:].bitcast(FP8X4),
                        rhs_scale=x_scale[c][:],
                        start=True,
                        stop=True,
                    )
                for u in range(share):
                    half, n = divmod(share * b + u, W3_HALF // P)
                    nc.tensor.matmul_mx(
                        out=y3[:, u * width : (u + 1) * width],
                        lhsT=w3_code[half][:, P * n : P * (n + 1)].bitcast(FP8X4),
                        lhsT_scale=w3_scale[half][:, P * n : P * (n + 1)],
                        rhs=x_code[c][:].bitcast(FP8X4),
                        rhs_scale=x_scale[c][:],
                        start=True,
                        stop=True,
                    )
                kept = ring.tile([P, BANK], F32, name=f"kept{c}_{b}", tag="kept", bufs=8)
                nc.scalar.copy(kept[:], y2[:])
                best = ring.tile([P, BANK], F32, name=f"best{c}_{b}", tag="best", bufs=6)
                nc.vector.tensor_tensor(best[:], y3[:], kept[:], ALU.max)
                nc.sync.dma_start(
                    out_rows[b][:, :, first : first + width], best[:].rearrange("p (u m) -> p u m", u=share)
                )

        fetch_after(0)
        group_x(0)
        for c in range(len(CHUNKS) + 1):
            if c + 1 < len(CHUNKS):
                fetch_after(c + 1)
            if c < len(CHUNKS):
                quantise_x(c)
            if c > 0:
                scores(c - 1)
            if c + 1 < len(CHUNKS):
                group_x(c + 1)
